import numpy as np
import ml_dtypes


def mxq(x, axis, fmt="e4m3"):
    dtype, down = {"e4m3": (ml_dtypes.float8_e4m3fn, 7), "e5m2": (ml_dtypes.float8_e5m2, 14)}[fmt]
    v = np.moveaxis(np.asarray(x, np.float32).astype(ml_dtypes.bfloat16).astype(np.float64), axis, -1)
    blocks = v.reshape(v.shape[:-1] + (-1, 32))
    amax = np.abs(blocks).max(-1, keepdims=True)
    byte = np.maximum(np.where(amax > 0, np.frexp(amax)[1] - 1 + 127, 0) - down, 1)
    scale = np.exp2(byte - 127.0)
    codes = (blocks / scale).astype(np.float32).astype(dtype).astype(np.float64)
    return np.moveaxis((codes * scale).reshape(v.shape), -1, axis)


WIDE = False


def mx_kscale(k, group=512):
    if not WIDE:
        return np.ones(k)
    levels = np.array([10, -10, 5, -5, 0])
    if group != 512:
        return np.exp2(np.random.permutation(np.resize(levels, k // group))).repeat(group)
    if k % 512:
        return np.exp2(np.random.permutation(np.resize(levels, k // 32))).repeat(32)
    a = np.empty((k // 512, 16))
    for p in range(k // 512):
        a[p, :8] = np.random.permutation(np.resize(levels, 8))
        for g in range(8):
            far = levels[np.abs(levels - a[p, g]) >= 10]
            a[p, g + 8] = far[np.random.randint(len(far))]
    return np.exp2(a.ravel()).repeat(32)


def f64(x):
    return np.asarray(x).astype(np.float64)


def striped(idx):
    return np.tile(np.asarray(idx).reshape(-1, 16).T, (8, 1)).astype(np.uint16)


def unstriped(offs):
    return offs[:16].T.reshape(-1).astype(np.int64)


H, KV, D, NQ, N = 4, 1, 256, 512, 512


def setup_inputs():
    n = np.random.standard_normal
    s = mx_kscale(D, 0)[:, None]
    u = mx_kscale(N)
    t = np.random.uniform(0.5, 2.0, N) * u
    v = n((KV, N, 128))
    return {
        "qT": (n((H, D, NQ)) * s * (0.70 / np.sqrt(D))).astype(np.float32),
        "kT": (n((KV, D, N)) / s).astype(np.float32),
        "t": t.reshape(N, 1).astype(np.float32),
        "v": (v / t[:, None]).astype(np.float32),
        "kb": (0.5 * n((N, 1))).astype(np.float32),
        "mask": (np.arange(N)[:, None] <= np.sort(np.random.randint(N // 4, N, NQ))[None, :]).astype(np.float32),
    }


def reference(qT, kT, t, v, kb, mask):
    a = np.repeat(mxq(f64(kT), 1, "e4m3"), H // KV, 0).transpose(0, 2, 1) @ mxq(f64(qT), 1, "e4m3")
    a = a + f64(kb)
    p = np.tanh(a)
    p = p * f64(mask)
    w = p * f64(t)
    y = mxq(w, 1, "e4m3").transpose(0, 2, 1) @ np.repeat(mxq(f64(v), 1, "e4m3"), H // KV, 0)
    y = y / 16.0
    return y

@@ -1,0 +1,233 @@
+from contextlib import ExitStack
+
+import concourse.mybir as mybir
+
+H, D, NQ, N, E = 4, 256, 512, 512, 128
+FLOPS = 2 * H * N * NQ * D + 2 * H * NQ * N * E
+
+F32 = mybir.dt.float32
+BF16 = mybir.dt.bfloat16
+U32 = mybir.dt.uint32
+U8 = mybir.dt.uint8
+FP8X4 = mybir.dt.float8_e4m3fn_x4
+ACT = mybir.ActivationFunctionType
+ALU = mybir.AluOpType
+
+P = 128
+PACK = 4
+ROWS = D // PACK
+HALF = NQ // 2
+COLS = 128
+RUN_W = 2
+RUN_Q = 4
+PV_LAG = 4
+OUT_LAG = 5
+
+
+def tile_rows_a_tanh_kb_mask_kernel(tc, qT, kT, t, v, kb, mask, out):
+    nc = tc.nc
+    with ExitStack() as ctx:
+        sb = ctx.enter_context(tc.tile_pool(name="sb", bufs=1))
+        ps = ctx.enter_context(tc.psum_pool(name="ps", bufs=1))
+        ctx.enter_context(tc.manual_schedule())
+
+        def alloc(name, shape, dtype):
+            return sb.tile(shape, dtype, name=name, align_bytes=64)
+
+        def quantize(name, grouped, words):
+            codes = alloc(name + "_codes", [P, words], U32)
+            scales = alloc(name + "_scales", [P, words], U8)
+            nc.vector.quantize_mx(
+                out=codes[:].bitcast(FP8X4),
+                scales=scales[:],
+                in_=grouped[:].rearrange("p w j -> p (w j)"),
+            )
+            return codes, scales
+
+        k_raw = alloc("k_raw", [P, PACK, N], F32)
+        k_rows = kT[0].rearrange("(p j) n -> p j n", j=PACK)
+        q_rows = [qT[2 * g : 2 * g + 2].rearrange("g (p j) q -> (g p) j q", j=PACK) for g in range(2)]
+        mask_rows = mask.rearrange("(p r) q -> p r q", r=PACK)
+        halves = [slice(a * HALF, (a + 1) * HALF) for a in range(2)]
+
+        nc.sync.dma_start(out=k_raw[0:ROWS], in_=k_rows)
+        nc.scalar.dma_start(out=k_raw[ROWS:P], in_=k_rows)
+        kb_sb = alloc("kb_sb", [P, PACK], F32)
+        t_sb = alloc("t_sb", [P, PACK], F32)
+        nc.scalar.dma_start(out=kb_sb[:], in_=kb.rearrange("(p r) o -> p (r o)", r=PACK))
+        nc.scalar.dma_start(out=t_sb[:], in_=t.rearrange("(p r) o -> p (r o)", r=PACK))
+        q0_raw, mask_raw = [], []
+        for a in range(2):
+            q0_raw.append(alloc("q0_raw%d" % a, [P, PACK, HALF], F32))
+            nc.sync.dma_start(out=q0_raw[a][:], in_=q_rows[0][:, :, halves[a]])
+            mask_raw.append(alloc("mask_raw%d" % a, [P, PACK, HALF], F32))
+            nc.sync.dma_start(out=mask_raw[a][:], in_=mask_rows[:, :, halves[a]])
+        q1_raw = alloc("q1_raw", [P, PACK, NQ], F32)
+        nc.sync.dma_start(out=q1_raw[:], in_=q_rows[1])
+        v_raw = alloc("v_raw", [P, PACK, E], F32)
+        nc.sync.dma_start(out=v_raw[:], in_=v[0].rearrange("(p r) e -> p r e", r=PACK))
+        q_raw = {(0, 0): q0_raw[0][:], (0, 1): q0_raw[1][:], (1, 0): q1_raw[:, :, halves[0]], (1, 1): q1_raw[:, :, halves[1]]}
+
+        warm = alloc("warm", [P, 1], F32)
+        warm_out = alloc("warm_out", [P, 1], F32)
+        nc.vector.memset(warm[:], 0.0)
+        nc.scalar.activation(out=warm_out[:], in_=warm[:], func=ACT.Tanh)
+
+        def interleave(copy, name, raw, width):
+            grouped = alloc(name, [P, width, PACK], BF16)
+            copy(
+                out=grouped[:].rearrange("p (c i) j -> p c j i", i=RUN_Q),
+                in_=raw.rearrange("p j (c i) -> p c j i", i=RUN_Q),
+            )
+            return grouped
+
+        k_grouped = alloc("k_grouped", [P, N, PACK], BF16)
+        nc.vector.tensor_copy(
+            out=k_grouped[:].rearrange("p (r s) j -> p s j r", r=PACK),
+            in_=k_raw[:].rearrange("p j (s r) -> p s j r", r=PACK),
+        )
+        k_codes, k_scales = quantize("k", k_grouped, N)
+
+        q_grouped, q_mx, mt = {}, {}, {}
+
+        def group_q(g, a, copy):
+            q_grouped[g, a] = alloc("q_grouped%d%d" % (g, a), [P, HALF, PACK], BF16)
+            copy(
+                out=q_grouped[g, a][:].rearrange("p (n c i) j -> p c j i n", n=2, i=2),
+                in_=q_raw[g, a].rearrange("p j (c i n) -> p c j i n", n=2, i=2),
+            )
+
+        def quantize_q(g, a):
+            q_mx[g, a] = quantize("q%d%d" % (g, a), q_grouped[g, a], HALF)
+
+        def make_mt(a):
+            mt[a] = alloc("mt%d" % a, [P, PACK, HALF], F32)
+            for r in range(PACK):
+                nc.vector.tensor_scalar(
+                    out=mt[a][:, r, :].rearrange("p (n m) -> p m n", n=2), in0=mask_raw[a][:, r, :].rearrange("p (m n) -> p m n", n=2), scalar1=t_sb[:, r : r + 1], scalar2=None, op0=ALU.mult
+                )
+
+        units = [(g, a, c) for g in range(2) for a in range(2) for c in range(2)]
+        score_banks = [[ps.tile([P, 2, HALF], F32, name="score%d%d" % (c, b)) for b in range(2)] for c in range(2)]
+        y_banks = [ps.tile([P, 2, 2, E], F32, name="y%d" % b) for b in range(4)]
+        p_tiles, w_tiles, w_mx = {}, {}, {}
+
+        def scores(u):
+            g, a, c = units[u]
+            rows = slice(c * ROWS, (c + 1) * ROWS)
+            codes, scales = q_mx[g, a]
+            for r in range(PACK):
+                for n in range(HALF // COLS):
+                    cols = slice(n * COLS, (n + 1) * COLS)
+                    tok = slice(r * P, (r + 1) * P)
+                    nc.tensor.matmul_mx(
+                        out=score_banks[c][r // 2][:, r % 2, cols],
+                        lhsT=k_codes[rows, tok].bitcast(FP8X4),
+                        lhsT_scale=k_scales[rows, tok],
+                        rhs=codes[rows, cols].bitcast(FP8X4),
+                        rhs_scale=scales[rows, cols],
+                        start=True,
+                        stop=True,
+                    )
+
+        def tanh(u):
+            g, a, c = units[u]
+            p_tiles[u] = alloc("p%d" % u, [P, PACK, HALF], F32)
+            for r in range(PACK):
+                nc.scalar.activation(
+                    out=p_tiles[u][:, r, :], in_=score_banks[c][r // 2][:, r % 2, :], func=ACT.Tanh, bias=kb_sb[:, r : r + 1]
+                )
+
+        def weigh(u):
+            g, a, c = units[u]
+            w_tiles[u] = alloc("w%d" % u, [P, HALF, PACK], BF16)
+            nc.vector.tensor_tensor(
+                out=w_tiles[u][:].rearrange("p (c i) r -> p c r i", i=RUN_W),
+                in0=p_tiles[u][:].rearrange("p r (c i) -> p c r i", i=RUN_W),
+                in1=mt[a][:].rearrange("p r (c i) -> p c r i", i=RUN_W),
+                op=ALU.mult,
+            )
+
+        def quantize_w(u):
+            w_mx[u] = quantize("w%d" % u, w_tiles[u], HALF)
+
+        def values(u):
+            codes, scales = w_mx[u]
+            for n in range(HALF // COLS):
+                cols = slice(n * COLS, (n + 1) * COLS)
+                nc.tensor.matmul_mx(
+                    out=y_banks[u % 4][:, u // 4, n, :],
+                    lhsT=codes[:, cols].bitcast(FP8X4),
+                    lhsT_scale=scales[:, cols],
+                    rhs=v_mx[0][:].bitcast(FP8X4),
+                    rhs_scale=v_mx[1][:],
+                    start=True,
+                    stop=True,
+                )
+
+        def store(u):
+            g, a, c = units[u]
+            y = alloc("y_sb%d" % u, [P, 2, E], F32)
+            nc.scalar.mul(out=y[:], in_=y_banks[u % 4][:, u // 4], mul=1.0 / 16.0)
+            nc.sync.dma_start(out=out[2 * g + c, halves[a], :].rearrange("(p n) e -> p n e", p=P), in_=y[:])
+
+        group_q(0, 0, nc.scalar.copy)
+        quantize_q(0, 0)
+        scores(0)
+        scores(1)
+        make_mt(0)
+        tanh(0)
+        group_q(0, 1, nc.vector.tensor_copy)
+        quantize_q(0, 1)
+        scores(2)
+        tanh(1)
+        scores(3)
+        weigh(0)
+        make_mt(1)
+        weigh(1)
+        tanh(2)
+        quantize_w(0)
+        group_q(1, 0, nc.scalar.copy)
+        weigh(2)
+        quantize_q(1, 0)
+        scores(4)
+        tanh(3)
+        quantize_w(1)
+        group_q(1, 1, nc.scalar.copy)
+        weigh(3)
+        quantize_q(1, 1)
+        scores(5)
+        tanh(4)
+        quantize_w(2)
+        v_grouped = interleave(nc.vector.tensor_copy, "v_grouped", v_raw[:], E)
+        scores(6)
+        tanh(5)
+        weigh(4)
+        v_mx = quantize("v", v_grouped, E)
+        values(0)
+        values(1)
+        values(2)
+        quantize_w(3)
+        scores(7)
+        values(3)
+        store(0)
+        store(1)
+        tanh(6)
+        weigh(5)
+        quantize_w(4)
+        values(4)
+        tanh(7)
+        store(2)
+        store(3)
+        weigh(6)
+        quantize_w(5)
+        values(5)
+        store(4)
+        store(5)
+        weigh(7)
+        quantize_w(6)
+        values(6)
+        store(6)
+        quantize_w(7)
+        values(7)
+        store(7)

@@ -9,6 +9,7 @@ F32 = mybir.dt.float32
 BF16 = mybir.dt.bfloat16
 U32 = mybir.dt.uint32
 U8 = mybir.dt.uint8
+I32 = mybir.dt.int32
 FP8X4 = mybir.dt.float8_e4m3fn_x4
 ACT = mybir.ActivationFunctionType
 ALU = mybir.AluOpType
@@ -44,29 +45,27 @@ def tile_rows_a_tanh_kb_mask_kernel(tc, qT, kT, t, v, kb, mask, out):
             )
             return codes, scales
 
-        k_raw = alloc("k_raw", [P, PACK, N], F32)
+        k_raw = alloc("k_raw", [ROWS, PACK, N], F32)
         k_rows = kT[0].rearrange("(p j) n -> p j n", j=PACK)
         q_rows = [qT[2 * g : 2 * g + 2].rearrange("g (p j) q -> (g p) j q", j=PACK) for g in range(2)]
         mask_rows = mask.rearrange("(p r) q -> p r q", r=PACK)
         halves = [slice(a * HALF, (a + 1) * HALF) for a in range(2)]
 
-        nc.sync.dma_start(out=k_raw[0:ROWS], in_=k_rows)
-        nc.scalar.dma_start(out=k_raw[ROWS:P], in_=k_rows)
+        nc.sync.dma_start(out=k_raw[:], in_=k_rows)
         kb_sb = alloc("kb_sb", [P, PACK], F32)
         t_sb = alloc("t_sb", [P, PACK], F32)
         nc.scalar.dma_start(out=kb_sb[:], in_=kb.rearrange("(p r) o -> p (r o)", r=PACK))
         nc.scalar.dma_start(out=t_sb[:], in_=t.rearrange("(p r) o -> p (r o)", r=PACK))
-        q0_raw, mask_raw = [], []
-        for a in range(2):
-            q0_raw.append(alloc("q0_raw%d" % a, [P, PACK, HALF], F32))
-            nc.sync.dma_start(out=q0_raw[a][:], in_=q_rows[0][:, :, halves[a]])
-            mask_raw.append(alloc("mask_raw%d" % a, [P, PACK, HALF], F32))
-            nc.sync.dma_start(out=mask_raw[a][:], in_=mask_rows[:, :, halves[a]])
+        q0_raw = alloc("q0_raw", [P, PACK, NQ], F32)
+        nc.sync.dma_start(out=q0_raw[:], in_=q_rows[0])
+        mask_all = alloc("mask_all", [P, PACK, NQ], F32)
+        nc.sync.dma_start(out=mask_all[:], in_=mask_rows)
+        mask_raw = [mask_all[:, :, halves[0]], mask_all[:, :, halves[1]]]
         q1_raw = alloc("q1_raw", [P, PACK, NQ], F32)
         nc.sync.dma_start(out=q1_raw[:], in_=q_rows[1])
         v_raw = alloc("v_raw", [P, PACK, E], F32)
         nc.sync.dma_start(out=v_raw[:], in_=v[0].rearrange("(p r) e -> p r e", r=PACK))
-        q_raw = {(0, 0): q0_raw[0][:], (0, 1): q0_raw[1][:], (1, 0): q1_raw[:, :, halves[0]], (1, 1): q1_raw[:, :, halves[1]]}
+        q_raw = {(0, 0): q0_raw[:, :, halves[0]], (0, 1): q0_raw[:, :, halves[1]], (1, 0): q1_raw[:, :, halves[0]], (1, 1): q1_raw[:, :, halves[1]]}
 
         warm = alloc("warm", [P, 1], F32)
         warm_out = alloc("warm_out", [P, 1], F32)
@@ -81,12 +80,19 @@ def tile_rows_a_tanh_kb_mask_kernel(tc, qT, kT, t, v, kb, mask, out):
             )
             return grouped
 
-        k_grouped = alloc("k_grouped", [P, N, PACK], BF16)
+        k_mx = [alloc("k_mx%d" % c, [P, N + N // PACK], U32) for c in range(2)]
+        nc.vector.memset(k_mx[0][0:ROWS, N:], 0)
+        k_grouped = alloc("k_grouped", [ROWS, N, PACK], BF16)
         nc.vector.tensor_copy(
             out=k_grouped[:].rearrange("p (r s) j -> p s j r", r=PACK),
             in_=k_raw[:].rearrange("p j (s r) -> p s j r", r=PACK),
         )
-        k_codes, k_scales = quantize("k", k_grouped, N)
+        nc.vector.quantize_mx(
+            out=k_mx[0][0:ROWS, 0:N].bitcast(FP8X4),
+            scales=k_mx[0][0:ROWS, N:].bitcast(U8),
+            in_=k_grouped[:].rearrange("p w j -> p (w j)"),
+        )
+        nc.scalar.dma_start(out=k_mx[1][ROWS:P, :].bitcast(I32), in_=k_mx[0][0:ROWS, :].bitcast(I32))
 
         q_grouped, q_mx, mt = {}, {}, {}
 
@@ -122,8 +128,8 @@ def tile_rows_a_tanh_kb_mask_kernel(tc, qT, kT, t, v, kb, mask, out):
                     tok = slice(r * P, (r + 1) * P)
                     nc.tensor.matmul_mx(
                         out=score_banks[c][r // 2][:, r % 2, cols],
-                        lhsT=k_codes[rows, tok].bitcast(FP8X4),
-                        lhsT_scale=k_scales[rows, tok],
+                        lhsT=k_mx[c][rows, tok].bitcast(FP8X4),
+                        lhsT_scale=k_mx[c][rows, N:].bitcast(U8)[:, tok],
                         rhs=codes[rows, cols].bitcast(FP8X4),
                         rhs_scale=scales[rows, cols],
                         start=True,
@@ -171,54 +177,54 @@ def tile_rows_a_tanh_kb_mask_kernel(tc, qT, kT, t, v, kb, mask, out):
             nc.scalar.mul(out=y[:], in_=y_banks[u % 4][:, u // 4], mul=1.0 / 16.0)
             nc.sync.dma_start(out=out[2 * g + c, halves[a], :].rearrange("(p n) e -> p n e", p=P), in_=y[:])
 
-        group_q(0, 0, nc.scalar.copy)
+        group_q(0, 0, nc.vector.tensor_copy)
+        group_q(0, 1, nc.scalar.copy)
         quantize_q(0, 0)
         scores(0)
         scores(1)
-        make_mt(0)
-        tanh(0)
-        group_q(0, 1, nc.vector.tensor_copy)
         quantize_q(0, 1)
+        make_mt(0)
+        make_mt(1)
+        tanh(0)
         scores(2)
         tanh(1)
         scores(3)
         weigh(0)
-        make_mt(1)
+        group_q(1, 0, nc.vector.tensor_copy)
         weigh(1)
-        tanh(2)
-        quantize_w(0)
-        group_q(1, 0, nc.scalar.copy)
-        weigh(2)
         quantize_q(1, 0)
+        tanh(2)
         scores(4)
+        quantize_w(0)
+        weigh(2)
         tanh(3)
-        quantize_w(1)
-        group_q(1, 1, nc.scalar.copy)
-        weigh(3)
-        quantize_q(1, 1)
+        group_q(1, 1, nc.vector.tensor_copy)
         scores(5)
+        quantize_w(1)
+        quantize_q(1, 1)
+        weigh(3)
         tanh(4)
-        quantize_w(2)
-        v_grouped = interleave(nc.vector.tensor_copy, "v_grouped", v_raw[:], E)
+        v_grouped = interleave(nc.scalar.copy, "v_grouped", v_raw[:], E)
         scores(6)
-        tanh(5)
+        quantize_w(2)
         weigh(4)
+        tanh(5)
+        scores(7)
         v_mx = quantize("v", v_grouped, E)
+        quantize_w(3)
         values(0)
         values(1)
         values(2)
-        quantize_w(3)
-        scores(7)
         values(3)
+        weigh(5)
+        tanh(6)
         store(0)
         store(1)
-        tanh(6)
-        weigh(5)
-        quantize_w(4)
-        values(4)
         tanh(7)
+        quantize_w(4)
         store(2)
         store(3)
+        values(4)
         weigh(6)
         quantize_w(5)
         values(5)

@@ -8,232 +8,209 @@ FLOPS = 2 * H * N * NQ * D + 2 * H * NQ * N * E
 F32 = mybir.dt.float32
 BF16 = mybir.dt.bfloat16
 U32 = mybir.dt.uint32
-U8 = mybir.dt.uint8
 I32 = mybir.dt.int32
+U8 = mybir.dt.uint8
 FP8X4 = mybir.dt.float8_e4m3fn_x4
-ACT = mybir.ActivationFunctionType
-ALU = mybir.AluOpType
 
 P = 128
 PACK = 4
 ROWS = D // PACK
 HALF = NQ // 2
 COLS = 128
-RUN_W = 2
-RUN_Q = 4
-PV_LAG = 4
-OUT_LAG = 5
+BLOCKS = HALF // COLS
+RUN = 4
+PLACES = 2
+FILLS_PER_UNIT = PACK // PLACES
+UNITS = [(g, a, c) for g in range(H // 2) for a in range(2) for c in range(2)]
+FILLS = len(UNITS) * FILLS_PER_UNIT
+SCORE_BANKS = 2 * FILLS_PER_UNIT
+Y_BANKS = 8 - SCORE_BANKS
+SECOND_PAIR = FILLS // 2
+OUT_SCALE = 1.0 / 16.0
 
 
 def tile_rows_a_tanh_kb_mask_kernel(tc, qT, kT, t, v, kb, mask, out):
     nc = tc.nc
     with ExitStack() as ctx:
-        sb = ctx.enter_context(tc.tile_pool(name="sb", bufs=1))
-        ps = ctx.enter_context(tc.psum_pool(name="ps", bufs=1))
+        sbuf = ctx.enter_context(tc.tile_pool(name="sbuf", bufs=1))
+        psum = ctx.enter_context(tc.psum_pool(name="psum", bufs=1))
         ctx.enter_context(tc.manual_schedule())
 
         def alloc(name, shape, dtype):
-            return sb.tile(shape, dtype, name=name, align_bytes=64)
+            return sbuf.tile(shape, dtype, name=name, align_bytes=64)
 
-        def quantize(name, grouped, words):
-            codes = alloc(name + "_codes", [P, words], U32)
-            scales = alloc(name + "_scales", [P, words], U8)
+        def load(queue, name, source):
+            raw = alloc(name, source.shape, F32)
+            queue.dma_start(out=raw[:], in_=source)
+            return raw
+
+        def quantize(name, grouped):
+            columns = grouped.shape[1]
+            codes = alloc(name + "_codes", [P, columns], U32)
+            scales = alloc(name + "_scales", [P, columns], U8)
             nc.vector.quantize_mx(
-                out=codes[:].bitcast(FP8X4),
-                scales=scales[:],
-                in_=grouped[:].rearrange("p w j -> p (w j)"),
+                out=codes[:].bitcast(FP8X4), scales=scales[:], in_=grouped[:].rearrange("p w j -> p (w j)")
             )
             return codes, scales
 
-        k_raw = alloc("k_raw", [ROWS, PACK, N], F32)
-        k_rows = kT[0].rearrange("(p j) n -> p j n", j=PACK)
-        q_rows = [qT[2 * g : 2 * g + 2].rearrange("g (p j) q -> (g p) j q", j=PACK) for g in range(2)]
-        mask_rows = mask.rearrange("(p r) q -> p r q", r=PACK)
-        halves = [slice(a * HALF, (a + 1) * HALF) for a in range(2)]
+        def q_rows(g):
+            return qT[2 * g : 2 * g + 2].rearrange("c (p j) q -> (c p) j q", j=PACK)
 
-        nc.sync.dma_start(out=k_raw[:], in_=k_rows)
-        kb_sb = alloc("kb_sb", [P, PACK], F32)
-        t_sb = alloc("t_sb", [P, PACK], F32)
-        nc.scalar.dma_start(out=kb_sb[:], in_=kb.rearrange("(p r) o -> p (r o)", r=PACK))
-        nc.scalar.dma_start(out=t_sb[:], in_=t.rearrange("(p r) o -> p (r o)", r=PACK))
-        q0_raw = alloc("q0_raw", [P, PACK, NQ], F32)
-        nc.sync.dma_start(out=q0_raw[:], in_=q_rows[0])
-        mask_all = alloc("mask_all", [P, PACK, NQ], F32)
-        nc.sync.dma_start(out=mask_all[:], in_=mask_rows)
-        mask_raw = [mask_all[:, :, halves[0]], mask_all[:, :, halves[1]]]
-        q1_raw = alloc("q1_raw", [P, PACK, NQ], F32)
-        nc.sync.dma_start(out=q1_raw[:], in_=q_rows[1])
-        v_raw = alloc("v_raw", [P, PACK, E], F32)
-        nc.sync.dma_start(out=v_raw[:], in_=v[0].rearrange("(p r) e -> p r e", r=PACK))
-        q_raw = {(0, 0): q0_raw[:, :, halves[0]], (0, 1): q0_raw[:, :, halves[1]], (1, 0): q1_raw[:, :, halves[0]], (1, 1): q1_raw[:, :, halves[1]]}
+        k_raw = load(nc.sync, "k_raw", kT[0].rearrange("(p j) i -> p j i", j=PACK))
+        kb_col = load(nc.scalar, "kb_col", kb.rearrange("(s r) o -> s (r o)", r=PACK))
+        t_col = load(nc.scalar, "t_col", t.rearrange("(s r) o -> s (r o)", r=PACK))
+        q_raw = [load(nc.sync, "q_raw0", q_rows(0))]
+        mask_raw = load(nc.sync, "mask_raw", mask.rearrange("(s r) q -> s r q", r=PACK))
 
-        warm = alloc("warm", [P, 1], F32)
-        warm_out = alloc("warm_out", [P, 1], F32)
-        nc.vector.memset(warm[:], 0.0)
-        nc.scalar.activation(out=warm_out[:], in_=warm[:], func=ACT.Tanh)
-
-        def interleave(copy, name, raw, width):
-            grouped = alloc(name, [P, width, PACK], BF16)
-            copy(
-                out=grouped[:].rearrange("p (c i) j -> p c j i", i=RUN_Q),
-                in_=raw.rearrange("p j (c i) -> p c j i", i=RUN_Q),
-            )
-            return grouped
-
-        k_mx = [alloc("k_mx%d" % c, [P, N + N // PACK], U32) for c in range(2)]
-        nc.vector.memset(k_mx[0][0:ROWS, N:], 0)
+        k_first = alloc("k_first", [ROWS, N + N // PACK], U32)
+        nc.vector.memset(k_first[:, N:], 0)
         k_grouped = alloc("k_grouped", [ROWS, N, PACK], BF16)
         nc.vector.tensor_copy(
             out=k_grouped[:].rearrange("p (r s) j -> p s j r", r=PACK),
             in_=k_raw[:].rearrange("p j (s r) -> p s j r", r=PACK),
         )
         nc.vector.quantize_mx(
-            out=k_mx[0][0:ROWS, 0:N].bitcast(FP8X4),
-            scales=k_mx[0][0:ROWS, N:].bitcast(U8),
+            out=k_first[:, 0:N].bitcast(FP8X4),
+            scales=k_first[:, N:].bitcast(U8),
             in_=k_grouped[:].rearrange("p w j -> p (w j)"),
         )
-        nc.scalar.dma_start(out=k_mx[1][ROWS:P, :].bitcast(I32), in_=k_mx[0][0:ROWS, :].bitcast(I32))
+        k_second = alloc("k_second", [P, N + N // PACK], U32)
+        nc.sync.dma_start(out=k_second[ROWS:P, :].bitcast(I32), in_=k_first[:].bitcast(I32))
+        k_mx = [k_first, k_second]
 
-        q_grouped, q_mx, mt = {}, {}, {}
+        v_raw = load(nc.sync, "v_raw", v[0].rearrange("(s r) e -> s r e", r=PACK))
+        q_raw.append(load(nc.sync, "q_raw1", q_rows(1)))
 
-        def group_q(g, a, copy):
-            q_grouped[g, a] = alloc("q_grouped%d%d" % (g, a), [P, HALF, PACK], BF16)
+        score_banks = [psum.tile([P, PLACES, HALF], F32, name="scores%d" % b) for b in range(SCORE_BANKS)]
+        y_banks = [psum.tile([P, 2, BLOCKS, E], F32, name="y%d" % b) for b in range(Y_BANKS)]
+        signed = [alloc("signed%d" % u, [P, PACK, HALF], F32) for u in range(len(UNITS))]
+        q_mx, w, w_mx = {}, {}, {}
+
+        def group_q(copy, g, a):
+            grouped = alloc("q_grouped%d%d" % (g, a), [P, HALF, PACK], BF16)
             copy(
-                out=q_grouped[g, a][:].rearrange("p (n c i) j -> p c j i n", n=2, i=2),
-                in_=q_raw[g, a].rearrange("p j (c i n) -> p c j i n", n=2, i=2),
+                out=grouped[:].rearrange("p (n grp col) j -> p grp j col n", n=BLOCKS, col=RUN // BLOCKS),
+                in_=q_raw[g][:, :, a * HALF : (a + 1) * HALF].rearrange(
+                    "p j (grp col n) -> p grp j col n", n=BLOCKS, col=RUN // BLOCKS
+                ),
             )
+            return grouped
 
-        def quantize_q(g, a):
-            q_mx[g, a] = quantize("q%d%d" % (g, a), q_grouped[g, a], HALF)
-
-        def make_mt(a):
-            mt[a] = alloc("mt%d" % a, [P, PACK, HALF], F32)
-            for r in range(PACK):
-                nc.vector.tensor_scalar(
-                    out=mt[a][:, r, :].rearrange("p (n m) -> p m n", n=2), in0=mask_raw[a][:, r, :].rearrange("p (m n) -> p m n", n=2), scalar1=t_sb[:, r : r + 1], scalar2=None, op0=ALU.mult
-                )
-
-        units = [(g, a, c) for g in range(2) for a in range(2) for c in range(2)]
-        score_banks = [[ps.tile([P, 2, HALF], F32, name="score%d%d" % (c, b)) for b in range(2)] for c in range(2)]
-        y_banks = [ps.tile([P, 2, 2, E], F32, name="y%d" % b) for b in range(4)]
-        p_tiles, w_tiles, w_mx = {}, {}, {}
-
-        def scores(u):
-            g, a, c = units[u]
+        def scores(f):
+            g, a, c = UNITS[f // FILLS_PER_UNIT]
             rows = slice(c * ROWS, (c + 1) * ROWS)
-            codes, scales = q_mx[g, a]
-            for r in range(PACK):
-                for n in range(HALF // COLS):
+            q_codes, q_scales = q_mx[g, a]
+            for x in range(PLACES):
+                r = f % FILLS_PER_UNIT * PLACES + x
+                tokens = slice(r * P, (r + 1) * P)
+                for n in range(BLOCKS):
                     cols = slice(n * COLS, (n + 1) * COLS)
-                    tok = slice(r * P, (r + 1) * P)
                     nc.tensor.matmul_mx(
-                        out=score_banks[c][r // 2][:, r % 2, cols],
-                        lhsT=k_mx[c][rows, tok].bitcast(FP8X4),
-                        lhsT_scale=k_mx[c][rows, N:].bitcast(U8)[:, tok],
-                        rhs=codes[rows, cols].bitcast(FP8X4),
-                        rhs_scale=scales[rows, cols],
+                        out=score_banks[f % SCORE_BANKS][:, x, cols],
+                        lhsT=k_mx[c][rows, tokens].bitcast(FP8X4),
+                        lhsT_scale=k_mx[c][rows, N:].bitcast(U8)[:, tokens],
+                        rhs=q_codes[rows, cols].bitcast(FP8X4),
+                        rhs_scale=q_scales[rows, cols],
                         start=True,
                         stop=True,
                     )
 
-        def tanh(u):
-            g, a, c = units[u]
-            p_tiles[u] = alloc("p%d" % u, [P, PACK, HALF], F32)
-            for r in range(PACK):
+        def tanh(f):
+            for x in range(PLACES):
+                r = f % FILLS_PER_UNIT * PLACES + x
                 nc.scalar.activation(
-                    out=p_tiles[u][:, r, :], in_=score_banks[c][r // 2][:, r % 2, :], func=ACT.Tanh, bias=kb_sb[:, r : r + 1]
+                    out=signed[f // FILLS_PER_UNIT][:, r, :],
+                    in_=score_banks[f % SCORE_BANKS][:, x, :],
+                    func=mybir.ActivationFunctionType.Tanh,
+                    bias=kb_col[:, r : r + 1],
                 )
 
         def weigh(u):
-            g, a, c = units[u]
-            w_tiles[u] = alloc("w%d" % u, [P, HALF, PACK], BF16)
+            a = UNITS[u][1]
+            w[u] = alloc("w%d" % u, [P, HALF, PACK], BF16)
             nc.vector.tensor_tensor(
-                out=w_tiles[u][:].rearrange("p (c i) r -> p c r i", i=RUN_W),
-                in0=p_tiles[u][:].rearrange("p r (c i) -> p c r i", i=RUN_W),
-                in1=mt[a][:].rearrange("p r (c i) -> p c r i", i=RUN_W),
-                op=ALU.mult,
+                out=w[u][:].rearrange("s (grp col) r -> s grp r col", col=RUN),
+                in0=signed[u][:].rearrange("s r (grp col) -> s grp r col", col=RUN),
+                in1=mask_t[:, :, a * HALF : (a + 1) * HALF].rearrange("s r (grp col) -> s grp r col", col=RUN),
+                op=mybir.AluOpType.mult,
             )
 
         def quantize_w(u):
-            w_mx[u] = quantize("w%d" % u, w_tiles[u], HALF)
+            w_mx[u] = quantize("w%d" % u, w[u])
 
-        def values(u):
-            codes, scales = w_mx[u]
-            for n in range(HALF // COLS):
+        def y_part(u):
+            if u < len(UNITS) // 2:
+                return y_banks[u // 2][:, u % 2]
+            return y_banks[Y_BANKS // 2 + u % 2][:, u // 2 % 2]
+
+        def second_product(u):
+            w_codes, w_scales = w_mx[u]
+            for n in range(BLOCKS):
                 cols = slice(n * COLS, (n + 1) * COLS)
                 nc.tensor.matmul_mx(
-                    out=y_banks[u % 4][:, u // 4, n, :],
-                    lhsT=codes[:, cols].bitcast(FP8X4),
-                    lhsT_scale=scales[:, cols],
-                    rhs=v_mx[0][:].bitcast(FP8X4),
-                    rhs_scale=v_mx[1][:],
+                    out=y_part(u)[:, n, :],
+                    lhsT=w_codes[:, cols].bitcast(FP8X4),
+                    lhsT_scale=w_scales[:, cols],
+                    rhs=v_codes[:].bitcast(FP8X4),
+                    rhs_scale=v_scales[:],
                     start=True,
                     stop=True,
                 )
 
         def store(u):
-            g, a, c = units[u]
-            y = alloc("y_sb%d" % u, [P, 2, E], F32)
-            nc.scalar.mul(out=y[:], in_=y_banks[u % 4][:, u // 4], mul=1.0 / 16.0)
-            nc.sync.dma_start(out=out[2 * g + c, halves[a], :].rearrange("(p n) e -> p n e", p=P), in_=y[:])
+            g, a, c = UNITS[u]
+            y = alloc("y_out%d" % u, [P, BLOCKS, E], F32)
+            nc.scalar.mul(out=y[:], in_=y_part(u), mul=OUT_SCALE)
+            rows = out[2 * g + c, a * HALF : (a + 1) * HALF, :]
+            nc.sync.dma_start(out=rows.rearrange("(m n) e -> m n e", n=BLOCKS), in_=y[:])
 
-        group_q(0, 0, nc.vector.tensor_copy)
-        group_q(0, 1, nc.scalar.copy)
-        quantize_q(0, 0)
-        scores(0)
-        scores(1)
-        quantize_q(0, 1)
-        make_mt(0)
-        make_mt(1)
-        tanh(0)
-        scores(2)
-        tanh(1)
-        scores(3)
-        weigh(0)
-        group_q(1, 0, nc.vector.tensor_copy)
-        weigh(1)
-        quantize_q(1, 0)
-        tanh(2)
-        scores(4)
-        quantize_w(0)
-        weigh(2)
-        tanh(3)
-        group_q(1, 1, nc.vector.tensor_copy)
-        scores(5)
-        quantize_w(1)
-        quantize_q(1, 1)
-        weigh(3)
-        tanh(4)
-        v_grouped = interleave(nc.scalar.copy, "v_grouped", v_raw[:], E)
-        scores(6)
-        quantize_w(2)
-        weigh(4)
-        tanh(5)
-        scores(7)
-        v_mx = quantize("v", v_grouped, E)
-        quantize_w(3)
-        values(0)
-        values(1)
-        values(2)
-        values(3)
-        weigh(5)
-        tanh(6)
-        store(0)
-        store(1)
-        tanh(7)
-        quantize_w(4)
-        store(2)
-        store(3)
-        values(4)
-        weigh(6)
-        quantize_w(5)
-        values(5)
-        store(4)
-        store(5)
-        weigh(7)
-        quantize_w(6)
-        values(6)
-        store(6)
-        quantize_w(7)
-        values(7)
-        store(7)
+        for a in range(2):
+            q_mx[0, a] = quantize("q0%d" % a, group_q(nc.vector.tensor_copy, 0, a))
+        for f in range(SCORE_BANKS):
+            scores(f)
+
+        mask_t = alloc("mask_t", [P, PACK, NQ], F32)
+        for r in range(PACK):
+            nc.vector.tensor_scalar(
+                out=mask_t[:, r, :].rearrange("s (a n m) -> s a m n", a=2, n=BLOCKS),
+                in0=mask_raw[:, r, :].rearrange("s (a m n) -> s a m n", a=2, n=BLOCKS),
+                scalar1=t_col[:, r : r + 1],
+                scalar2=None,
+                op0=mybir.AluOpType.mult,
+            )
+
+        last = len(UNITS) - 1
+        last_scores = (FILLS - 1 - SCORE_BANKS) // FILLS_PER_UNIT
+        for u in range(len(UNITS)):
+            for f in range(u * FILLS_PER_UNIT, (u + 1) * FILLS_PER_UNIT):
+                tanh(f)
+                ahead = f + SCORE_BANKS
+                if ahead == SECOND_PAIR:
+                    halves = [group_q(nc.scalar.copy, 1, 0), group_q(nc.vector.tensor_copy, 1, 1)]
+                    for a in range(2):
+                        q_mx[1, a] = quantize("q1%d" % a, halves[a])
+                if ahead < FILLS:
+                    scores(ahead)
+            if u == last:
+                for done in range(last - 1):
+                    store(done)
+            weigh(u)
+            if u == 0:
+                v_grouped = alloc("v_grouped", [P, E, PACK], BF16)
+                nc.vector.tensor_copy(
+                    out=v_grouped[:].rearrange("s (grp col) r -> s grp r col", col=RUN),
+                    in_=v_raw[:].rearrange("s r (grp col) -> s grp r col", col=RUN),
+                )
+                continue
+            if u == 1:
+                v_codes, v_scales = quantize("v", v_grouped)
+            quantize_w(u - 1)
+            if u == last_scores:
+                for earlier in range(u - 1):
+                    second_product(earlier)
+            if u >= last_scores:
+                second_product(u - 1)
+        store(last - 1)
+        quantize_w(last)
+        second_product(last)
+        store(last)

from contextlib import ExitStack

import concourse.mybir as mybir

H, D, NQ, N, E = 4, 256, 512, 512, 128
FLOPS = 2 * H * N * NQ * D + 2 * H * NQ * N * E

F32 = mybir.dt.float32
BF16 = mybir.dt.bfloat16
U32 = mybir.dt.uint32
I32 = mybir.dt.int32
U8 = mybir.dt.uint8
FP8X4 = mybir.dt.float8_e4m3fn_x4

P = 128
PACK = 4
ROWS = D // PACK
HALF = NQ // 2
COLS = 128
BLOCKS = HALF // COLS
RUN = 4
PLACES = 2
FILLS_PER_UNIT = PACK // PLACES
UNITS = [(g, a, c) for g in range(H // 2) for a in range(2) for c in range(2)]
FILLS = len(UNITS) * FILLS_PER_UNIT
SCORE_BANKS = 2 * FILLS_PER_UNIT
Y_BANKS = 8 - SCORE_BANKS
SECOND_PAIR = FILLS // 2
OUT_SCALE = 1.0 / 16.0


def tile_rows_a_tanh_kb_mask_kernel(tc, qT, kT, t, v, kb, mask, out):
    nc = tc.nc
    with ExitStack() as ctx:
        sbuf = ctx.enter_context(tc.tile_pool(name="sbuf", bufs=1))
        psum = ctx.enter_context(tc.psum_pool(name="psum", bufs=1))
        ctx.enter_context(tc.manual_schedule())

        def alloc(name, shape, dtype):
            return sbuf.tile(shape, dtype, name=name, align_bytes=64)

        def load(queue, name, source):
            raw = alloc(name, source.shape, F32)
            queue.dma_start(out=raw[:], in_=source)
            return raw

        def quantize(name, grouped):
            columns = grouped.shape[1]
            codes = alloc(name + "_codes", [P, columns], U32)
            scales = alloc(name + "_scales", [P, columns], U8)
            nc.vector.quantize_mx(
                out=codes[:].bitcast(FP8X4), scales=scales[:], in_=grouped[:].rearrange("p w j -> p (w j)")
            )
            return codes, scales

        def q_rows(g):
            return qT[2 * g : 2 * g + 2].rearrange("c (p j) q -> (c p) j q", j=PACK)

        k_raw = load(nc.sync, "k_raw", kT[0].rearrange("(p j) i -> p j i", j=PACK))
        kb_col = load(nc.scalar, "kb_col", kb.rearrange("(s r) o -> s (r o)", r=PACK))
        t_col = load(nc.scalar, "t_col", t.rearrange("(s r) o -> s (r o)", r=PACK))
        q_raw = [load(nc.sync, "q_raw0", q_rows(0))]
        mask_raw = load(nc.sync, "mask_raw", mask.rearrange("(s r) q -> s r q", r=PACK))

        k_first = alloc("k_first", [ROWS, N + N // PACK], U32)
        nc.vector.memset(k_first[:, N:], 0)
        k_grouped = alloc("k_grouped", [ROWS, N, PACK], BF16)
        nc.vector.tensor_copy(
            out=k_grouped[:].rearrange("p (r s) j -> p s j r", r=PACK),
            in_=k_raw[:].rearrange("p j (s r) -> p s j r", r=PACK),
        )
        nc.vector.quantize_mx(
            out=k_first[:, 0:N].bitcast(FP8X4),
            scales=k_first[:, N:].bitcast(U8),
            in_=k_grouped[:].rearrange("p w j -> p (w j)"),
        )
        k_second = alloc("k_second", [P, N + N // PACK], U32)
        nc.sync.dma_start(out=k_second[ROWS:P, :].bitcast(I32), in_=k_first[:].bitcast(I32))
        k_mx = [k_first, k_second]

        v_raw = load(nc.sync, "v_raw", v[0].rearrange("(s r) e -> s r e", r=PACK))
        q_raw.append(load(nc.sync, "q_raw1", q_rows(1)))

        score_banks = [psum.tile([P, PLACES, HALF], F32, name="scores%d" % b) for b in range(SCORE_BANKS)]
        y_banks = [psum.tile([P, 2, BLOCKS, E], F32, name="y%d" % b) for b in range(Y_BANKS)]
        signed = [alloc("signed%d" % u, [P, PACK, HALF], F32) for u in range(len(UNITS))]
        q_mx, w, w_mx = {}, {}, {}

        def group_q(copy, g, a):
            grouped = alloc("q_grouped%d%d" % (g, a), [P, HALF, PACK], BF16)
            copy(
                out=grouped[:].rearrange("p (n grp col) j -> p grp j col n", n=BLOCKS, col=RUN // BLOCKS),
                in_=q_raw[g][:, :, a * HALF : (a + 1) * HALF].rearrange(
                    "p j (grp col n) -> p grp j col n", n=BLOCKS, col=RUN // BLOCKS
                ),
            )
            return grouped

        def scores(f):
            g, a, c = UNITS[f // FILLS_PER_UNIT]
            rows = slice(c * ROWS, (c + 1) * ROWS)
            q_codes, q_scales = q_mx[g, a]
            for x in range(PLACES):
                r = f % FILLS_PER_UNIT * PLACES + x
                tokens = slice(r * P, (r + 1) * P)
                for n in range(BLOCKS):
                    cols = slice(n * COLS, (n + 1) * COLS)
                    nc.tensor.matmul_mx(
                        out=score_banks[f % SCORE_BANKS][:, x, cols],
                        lhsT=k_mx[c][rows, tokens].bitcast(FP8X4),
                        lhsT_scale=k_mx[c][rows, N:].bitcast(U8)[:, tokens],
                        rhs=q_codes[rows, cols].bitcast(FP8X4),
                        rhs_scale=q_scales[rows, cols],
                        start=True,
                        stop=True,
                    )

        def tanh(f):
            for x in range(PLACES):
                r = f % FILLS_PER_UNIT * PLACES + x
                nc.scalar.activation(
                    out=signed[f // FILLS_PER_UNIT][:, r, :],
                    in_=score_banks[f % SCORE_BANKS][:, x, :],
                    func=mybir.ActivationFunctionType.Tanh,
                    bias=kb_col[:, r : r + 1],
                )

        def weigh(u):
            a = UNITS[u][1]
            w[u] = alloc("w%d" % u, [P, HALF, PACK], BF16)
            nc.vector.tensor_tensor(
                out=w[u][:].rearrange("s (grp col) r -> s grp r col", col=RUN),
                in0=signed[u][:].rearrange("s r (grp col) -> s grp r col", col=RUN),
                in1=mask_t[:, :, a * HALF : (a + 1) * HALF].rearrange("s r (grp col) -> s grp r col", col=RUN),
                op=mybir.AluOpType.mult,
            )

        def quantize_w(u):
            w_mx[u] = quantize("w%d" % u, w[u])

        def y_part(u):
            if u < len(UNITS) // 2:
                return y_banks[u // 2][:, u % 2]
            return y_banks[Y_BANKS // 2 + u % 2][:, u // 2 % 2]

        def second_product(u):
            w_codes, w_scales = w_mx[u]
            for n in range(BLOCKS):
                cols = slice(n * COLS, (n + 1) * COLS)
                nc.tensor.matmul_mx(
                    out=y_part(u)[:, n, :],
                    lhsT=w_codes[:, cols].bitcast(FP8X4),
                    lhsT_scale=w_scales[:, cols],
                    rhs=v_codes[:].bitcast(FP8X4),
                    rhs_scale=v_scales[:],
                    start=True,
                    stop=True,
                )

        def store(u):
            g, a, c = UNITS[u]
            y = alloc("y_out%d" % u, [P, BLOCKS, E], F32)
            nc.scalar.mul(out=y[:], in_=y_part(u), mul=OUT_SCALE)
            rows = out[2 * g + c, a * HALF : (a + 1) * HALF, :]
            nc.sync.dma_start(out=rows.rearrange("(m n) e -> m n e", n=BLOCKS), in_=y[:])

        for a in range(2):
            q_mx[0, a] = quantize("q0%d" % a, group_q(nc.vector.tensor_copy, 0, a))
        for f in range(SCORE_BANKS):
            scores(f)

        mask_t = alloc("mask_t", [P, PACK, NQ], F32)
        for r in range(PACK):
            nc.vector.tensor_scalar(
                out=mask_t[:, r, :].rearrange("s (a n m) -> s a m n", a=2, n=BLOCKS),
                in0=mask_raw[:, r, :].rearrange("s (a m n) -> s a m n", a=2, n=BLOCKS),
                scalar1=t_col[:, r : r + 1],
                scalar2=None,
                op0=mybir.AluOpType.mult,
            )

        last = len(UNITS) - 1
        last_scores = (FILLS - 1 - SCORE_BANKS) // FILLS_PER_UNIT
        for u in range(len(UNITS)):
            for f in range(u * FILLS_PER_UNIT, (u + 1) * FILLS_PER_UNIT):
                tanh(f)
                ahead = f + SCORE_BANKS
                if ahead == SECOND_PAIR:
                    halves = [group_q(nc.scalar.copy, 1, 0), group_q(nc.vector.tensor_copy, 1, 1)]
                    for a in range(2):
                        q_mx[1, a] = quantize("q1%d" % a, halves[a])
                if ahead < FILLS:
                    scores(ahead)
            if u == last:
                for done in range(last - 1):
                    store(done)
            weigh(u)
            if u == 0:
                v_grouped = alloc("v_grouped", [P, E, PACK], BF16)
                nc.vector.tensor_copy(
                    out=v_grouped[:].rearrange("s (grp col) r -> s grp r col", col=RUN),
                    in_=v_raw[:].rearrange("s r (grp col) -> s grp r col", col=RUN),
                )
                continue
            if u == 1:
                v_codes, v_scales = quantize("v", v_grouped)
            quantize_w(u - 1)
            if u == last_scores:
                for earlier in range(u - 1):
                    second_product(earlier)
            if u >= last_scores:
                second_product(u - 1)
        store(last - 1)
        quantize_w(last)
        second_product(last)
        store(last)
